import numpy as np
import ml_dtypes

BF16 = ml_dtypes.bfloat16


def bf(x):
    return np.asarray(x, np.float32).astype(BF16)


def f32(x):
    return np.asarray(x, np.float32)


def f64(x):
    return np.asarray(x).astype(np.float64)


def striped(idx):
    return np.tile(idx.reshape(-1, 16).T, (8, 1))


S, K, M, N, H = 1024, 512, 256, 128, 128


def sigmoid(v):
    return 1.0 / (1.0 + np.exp(-v))


def setup_inputs():
    return {"table": bf(np.random.standard_normal((K, S))), "w": bf(np.random.standard_normal((K, M)) / np.sqrt(K)), "offs": striped(np.sort(np.random.permutation(S)[:N]))}


def reference(table, w, offs):
    idx = offs[:16].T.reshape(-1)
    x = f64(table)[:, idx]
    y = f64(w).T @ x
    return y[:H] * sigmoid(y[H:])

@@ -1,0 +1,49 @@
+import concourse.mybir as mybir
+
+BF16, F32, U16 = mybir.dt.bfloat16, mybir.dt.float32, mybir.dt.uint16
+SIGMOID = mybir.ActivationFunctionType.Sigmoid
+MULT = mybir.AluOpType.mult
+
+P = 128
+K = 512
+S = 1024
+N = 128
+H = 128
+KB = K // P
+
+FLOPS = 2 * K * (2 * H) * N
+
+
+def tile_gather_matmul_kernel(tc, table, w, offs, out):
+    nc = tc.nc
+    with (
+        tc.tile_pool(name="held", bufs=1) as held,
+        tc.psum_pool(name="psum", bufs=1) as psum,
+    ):
+        offsets = held.tile([P, N // 16], U16, name="offsets")
+        nc.sync.dma_start(offsets[:], offs)
+
+        weights = held.tile([P, KB, 2 * H], BF16, name="weights")
+        nc.scalar.dma_start(weights[:], w.rearrange("(p b) m -> p b m", b=KB))
+
+        by_block = table.rearrange("(p b) s -> b p s", b=KB)
+        blocks = []
+        for b in range(KB):
+            block = held.tile([P, S], BF16, name=f"block{b}")
+            starter = nc.sync if b % 2 == 0 else nc.scalar
+            starter.dma_start(block[:], by_block[b])
+            blocks.append(block)
+
+        gate = psum.tile([H, N], F32, name="gate")
+        value = psum.tile([H, N], F32, name="value")
+        for b in range(KB):
+            picked = blocks[b][:].indirect(offsets[:])
+            first, last = b == 0, b == KB - 1
+            nc.tensor.matmul(gate[:], weights[:, b, H : 2 * H], picked, start=first, stop=last)
+            nc.tensor.matmul(value[:], weights[:, b, 0:H], picked, start=first, stop=last)
+
+        opened = held.tile([H, N], F32, name="opened")
+        nc.scalar.activation(opened[:], gate[:], SIGMOID)
+        result = held.tile([H, N], F32, name="result")
+        nc.vector.tensor_tensor(result[:], value[:], opened[:], MULT)
+        nc.sync.dma_start(out, result[:])

@@ -43,7 +43,10 @@ def tile_gather_matmul_kernel(tc, table, w, offs, out):
             nc.tensor.matmul(value[:], weights[:, b, 0:H], picked, start=first, stop=last)
 
         opened = held.tile([H, N], F32, name="opened")
-        nc.scalar.activation(opened[:], gate[:], SIGMOID)
         result = held.tile([H, N], F32, name="result")
-        nc.vector.tensor_tensor(result[:], value[:], opened[:], MULT)
-        nc.sync.dma_start(out, result[:])
+        for half in range(2):
+            cols = slice(half * (N // 2), (half + 1) * (N // 2))
+            nc.scalar.activation(opened[:, cols], gate[:, cols], SIGMOID)
+            nc.vector.tensor_tensor(result[:, cols], value[:, cols], opened[:, cols], MULT)
+            starter = nc.sync if half == 0 else nc.scalar
+            starter.dma_start(out[:, cols], result[:, cols])

@@ -21,7 +21,6 @@ def tile_gather_matmul_kernel(tc, table, w, offs, out):
         tc.psum_pool(name="psum", bufs=1) as psum,
     ):
         offsets = held.tile([P, N // 16], U16, name="offsets")
-        nc.sync.dma_start(offsets[:], offs)
 
         weights = held.tile([P, KB, 2 * H], BF16, name="weights")
         nc.scalar.dma_start(weights[:], w.rearrange("(p b) m -> p b m", b=KB))
@@ -33,6 +32,8 @@ def tile_gather_matmul_kernel(tc, table, w, offs, out):
             starter = nc.sync if b % 2 == 0 else nc.scalar
             starter.dma_start(block[:], by_block[b])
             blocks.append(block)
+            if b == 0:
+                nc.sync.dma_start(offsets[:], offs)
 
         gate = psum.tile([H, N], F32, name="gate")
         value = psum.tile([H, N], F32, name="value")

import concourse.mybir as mybir

BF16, F32, U16 = mybir.dt.bfloat16, mybir.dt.float32, mybir.dt.uint16
SIGMOID = mybir.ActivationFunctionType.Sigmoid
MULT = mybir.AluOpType.mult

P = 128
K = 512
S = 1024
N = 128
H = 128
KB = K // P

FLOPS = 2 * K * (2 * H) * N


def tile_gather_matmul_kernel(tc, table, w, offs, out):
    nc = tc.nc
    with (
        tc.tile_pool(name="held", bufs=1) as held,
        tc.psum_pool(name="psum", bufs=1) as psum,
    ):
        offsets = held.tile([P, N // 16], U16, name="offsets")

        weights = held.tile([P, KB, 2 * H], BF16, name="weights")
        nc.scalar.dma_start(weights[:], w.rearrange("(p b) m -> p b m", b=KB))

        by_block = table.rearrange("(p b) s -> b p s", b=KB)
        blocks = []
        for b in range(KB):
            block = held.tile([P, S], BF16, name=f"block{b}")
            starter = nc.sync if b % 2 == 0 else nc.scalar
            starter.dma_start(block[:], by_block[b])
            blocks.append(block)
            if b == 0:
                nc.sync.dma_start(offsets[:], offs)

        gate = psum.tile([H, N], F32, name="gate")
        value = psum.tile([H, N], F32, name="value")
        for b in range(KB):
            picked = blocks[b][:].indirect(offsets[:])
            first, last = b == 0, b == KB - 1
            nc.tensor.matmul(gate[:], weights[:, b, H : 2 * H], picked, start=first, stop=last)
            nc.tensor.matmul(value[:], weights[:, b, 0:H], picked, start=first, stop=last)

        opened = held.tile([H, N], F32, name="opened")
        result = held.tile([H, N], F32, name="result")
        for half in range(2):
            cols = slice(half * (N // 2), (half + 1) * (N // 2))
            nc.scalar.activation(opened[:, cols], gate[:, cols], SIGMOID)
            nc.vector.tensor_tensor(result[:, cols], value[:, cols], opened[:, cols], MULT)
            starter = nc.sync if half == 0 else nc.scalar
            starter.dma_start(out[:, cols], result[:, cols])
